import numpy as np
import ml_dtypes


def mxq(x, axis, fmt="e4m3"):
    dtype, down = {"e4m3": (ml_dtypes.float8_e4m3fn, 7), "e5m2": (ml_dtypes.float8_e5m2, 14)}[fmt]
    v = np.moveaxis(np.asarray(x, np.float32).astype(ml_dtypes.bfloat16).astype(np.float64), axis, -1)
    blocks = v.reshape(v.shape[:-1] + (-1, 32))
    amax = np.abs(blocks).max(-1, keepdims=True)
    byte = np.maximum(np.where(amax > 0, np.frexp(amax)[1] - 1 + 127, 0) - down, 1)
    scale = np.exp2(byte - 127.0)
    codes = (blocks / scale).astype(np.float32).astype(dtype).astype(np.float64)
    return np.moveaxis((codes * scale).reshape(v.shape), -1, axis)


WIDE = False


def mx_kscale(k):
    if not WIDE:
        return np.ones(k)
    levels = np.array([10, -10, 5, -5, 0])
    if k % 512:
        return np.exp2(np.random.permutation(np.resize(levels, k // 32))).repeat(32)
    a = np.empty((k // 512, 16))
    for p in range(k // 512):
        a[p, :8] = np.random.permutation(np.resize(levels, 8))
        for g in range(8):
            far = levels[np.abs(levels - a[p, g]) >= 10]
            a[p, g + 8] = far[np.random.randint(len(far))]
    return np.exp2(a.ravel()).repeat(32)


def f64(x):
    return np.asarray(x).astype(np.float64)


def striped(idx):
    return np.tile(idx.reshape(-1, 16).T, (8, 1)).astype(np.uint16)


def unstriped(offs):
    return offs[:16].T.reshape(-1).astype(np.int64)


def pack_weight(w):
    k, n = w.shape
    w = f64(np.asarray(w, np.float32).astype(ml_dtypes.bfloat16)).reshape(k // 32, 32, n)
    amax = np.abs(w).max(1)
    byte = np.clip(np.where(amax > 0, np.frexp(amax)[1] - 1 + 127 - 7, 1), 1, 254)
    scaled = (w * np.exp2(127.0 - byte)[:, None, :]).reshape(k, n).astype(np.float32)
    words = np.ascontiguousarray(scaled.reshape(k // 512, 128, 4, n).transpose(0, 1, 3, 2)).astype(ml_dtypes.float8_e4m3fn).view(np.uint8)
    return words, np.ascontiguousarray(byte.astype(np.uint8).reshape(k // 512, 16, n))


def unpack_weight(words, scales):
    g, p, n, _ = words.shape
    vals = np.ascontiguousarray(words).view(ml_dtypes.float8_e4m3fn).astype(np.float64) * np.repeat(np.exp2(scales.astype(np.float64) - 127.0), 8, axis=1)[..., None]
    return vals.transpose(0, 1, 3, 2).reshape(g * 512, n)


def sigmoid(v):
    return 1.0 / (1.0 + np.exp(-np.maximum(v, -700.0)))


K, T, S, H, W, C, U = 512, 2048, 256, 512, 128, 512, 512


def setup_inputs():
    n = np.random.standard_normal
    s = mx_kscale(K)[:, None]
    packed_xT = pack_weight(n((K, T)) * s)
    packed_w1 = pack_weight(n((K, H)) / np.sqrt(2 * K) / s)
    packed_w2 = pack_weight(n((K, H)) / np.sqrt(2 * K) / s)
    perm = np.random.permutation(U)
    return {
        "x_words": packed_xT[0],
        "x_scales": packed_xT[1],
        "w1_words": packed_w1[0],
        "w1_scales": packed_w1[1],
        "w2_words": packed_w2[0],
        "w2_scales": packed_w2[1],
        "gs": (np.random.uniform(0.5, 1.5, (K, 1)) / s).astype(np.float32),
        "sl": np.random.uniform(1.0, 2.0, (C, 1)).astype(np.float32),
        "th": (0.5 * n((C, 1))).astype(np.float32),
        "offs": striped(np.random.permutation(T)[:S]),
        "two": striped(np.random.permutation(T)[:S]),
        "n1": striped(np.random.permutation(S)[:W]),
        "n2": striped(np.random.permutation(S)[:W]),
        "n3": striped(np.random.permutation(S)),
        "cand": striped(np.random.permutation(T)[:C]),
        "n4": striped(perm[:S]),
        "n5": striped(perm[S:]),
        "n6": striped(np.random.permutation(S)),
    }


def reference(x_words, x_scales, w1_words, w1_scales, w2_words, w2_scales, gs, sl, th, offs, two, n1, n2, n3, cand, n4, n5, n6):
    x_cand = unpack_weight(x_words, x_scales)[:, unstriped(cand)]
    xq = unpack_weight(x_words, x_scales)[:, unstriped(offs)]
    x_two = unpack_weight(x_words, x_scales)[:, unstriped(two)]
    y = unpack_weight(w1_words, w1_scales).T @ xq + unpack_weight(w2_words, w2_scales).T @ x_two
    pa = y[:, unstriped(n2)]
    ds = y.copy()
    ds[:, unstriped(n1)] = pa
    z = f64(gs) * (ds - (0.5 * ds[:, unstriped(n3)]))
    s = 0.0625 * ((x_cand.T @ mxq(z, 0, "e4m3")))
    sg = sigmoid(f64(sl) * (s[:, unstriped(n6)] - f64(th)))
    st = s * sg
    ph = np.zeros((C, U))
    ph[:, unstriped(n4)] = s
    out = ph.copy()
    out[:, unstriped(n5)] = st
    return out

@@ -1,0 +1,177 @@
+from contextlib import ExitStack
+
+import concourse.mybir as mybir
+
+K, T, S, H, W, C, U = 512, 2048, 256, 512, 128, 512, 512
+FLOPS = 2 * K * S * (2 * H + C)
+
+F32 = mybir.dt.float32
+BF16 = mybir.dt.bfloat16
+I32 = mybir.dt.int32
+U32 = mybir.dt.uint32
+U16 = mybir.dt.uint16
+U8 = mybir.dt.uint8
+FP8X4 = mybir.dt.float8_e4m3fn_x4
+ALU = mybir.AluOpType
+ACT = mybir.ActivationFunctionType
+
+P = 128
+PACK = 4
+QUADS = 4
+QUAD = 32
+HALF = S // 2
+LIST_COL = 16
+PIECES = ((0, 128), (128, 256))
+
+
+def tile_picked_dttzcksetepag_none_p_kernel(
+    tc, x_words, x_scales, w1_words, w1_scales, w2_words, w2_scales, gs, sl, th,
+    offs, two, n1, n2, n3, cand, n4, n5, n6, out,
+):
+    nc = tc.nc
+
+    with ExitStack() as ctx:
+        keep = ctx.enter_context(tc.tile_pool(name="keep", bufs=1))
+        psum = ctx.enter_context(tc.psum_pool(name="psum", bufs=1))
+
+        def load_list(src, name):
+            tile = keep.tile(list(src.shape), U16, name=name)
+            nc.sync.dma_start(tile[:], src)
+            return tile
+
+        def load_words(src, name):
+            tile = keep.tile([P, src.shape[2]], U32, name=name, align_bytes=64)
+            nc.sync.dma_start(tile[:].bitcast(I32), src[0].rearrange("p n t -> p (n t)").bitcast(I32))
+            return tile
+
+        def load_scale_rows(queue, tile, src, first, quads):
+            for q in quads:
+                rows = tile[QUAD * q + first : QUAD * q + first + 4, :]
+                queue.dma_start(rows.bitcast(I32), src[0, 4 * q : 4 * q + 4, :].bitcast(I32))
+
+        def part(lst, j0, j1):
+            return lst[:, j0 // LIST_COL : j1 // LIST_COL]
+
+        xs = keep.tile([P, T], U8, align_bytes=64)
+        ws = keep.tile([P, H], U8, align_bytes=64)
+        nc.vector.memset(xs[:].bitcast(I32), 0)
+        nc.vector.memset(ws[:].bitcast(I32), 0)
+
+        load_scale_rows(nc.sync, xs, x_scales, 0, range(QUADS))
+        offs_t = load_list(offs, "offs_t")
+        two_t = load_list(two, "two_t")
+        gs_t = keep.tile([P, PACK], F32)
+        nc.sync.dma_start(gs_t[:], gs.rearrange("(p t) o -> p (t o)", t=PACK))
+        xw = load_words(x_words, "xw")
+        load_scale_rows(nc.sync, ws, w1_scales, 0, range(QUADS))
+        w1 = load_words(w1_words, "w1")
+        load_scale_rows(nc.sync, ws, w2_scales, 4, range(1))
+        load_scale_rows(nc.gpsimd, ws, w2_scales, 4, range(1, QUADS))
+        w2 = load_words(w2_words, "w2")
+        n2_t = load_list(n2, "n2_t")
+        n1_t = load_list(n1, "n1_t")
+        n3_t = load_list(n3, "n3_t")
+        cand_t = load_list(cand, "cand_t")
+        n4_t = load_list(n4, "n4_t")
+        n6_t = load_list(n6, "n6_t")
+        n5_t = load_list(n5, "n5_t")
+        sl_t = keep.tile([P, C // P], F32)
+        th_t = keep.tile([P, C // P], F32)
+        with nc.allow_non_contiguous_dma(reason="one value a partition for each block of rows"):
+            nc.sync.dma_start(sl_t[:], sl.rearrange("(c p) o -> p (c o)", p=P))
+            nc.sync.dma_start(th_t[:], th.rearrange("(c p) o -> p (c o)", p=P))
+
+        def pick(lst, n, name, tag):
+            scales = keep.tile([P, n], U8, name=name + "_scales", tag=tag + "_scales", align_bytes=64)
+            words = keep.tile([P, n], U32, name=name + "_words", tag=tag + "_words", align_bytes=64)
+            nc.vector.tensor_copy(scales[:], xs[:].indirect(lst[:]))
+            nc.vector.tensor_copy(words[:], xw[:].indirect(lst[:]))
+            return words, scales
+
+        xq_w, xq_s = pick(offs_t, S, "xq", "first")
+        xt_w, xt_s = pick(two_t, S, "xt", "second")
+
+        ws_d = keep.tile([P, H], U8, align_bytes=64)
+        w1_d = keep.tile([P, H], U32, align_bytes=64)
+        w2_d = keep.tile([P, H], U32, align_bytes=64)
+
+        def deal(copy, dst, src, t0, t1):
+            copy(dst[:].rearrange("p (t m) -> p t m", t=PACK)[:, t0:t1, :], src[:].rearrange("p (m t) -> p t m", t=PACK)[:, t0:t1, :])
+
+        nc.scalar.copy(w1_d[:].rearrange("p (t m) -> p m t", t=PACK), w1[:].rearrange("p (m t) -> p m t", t=PACK))
+        for t0, t1 in ((0, 1), (1, PACK)):
+            deal(nc.vector.tensor_copy, ws_d, ws, t0, t1)
+            deal(nc.scalar.copy, w2_d, w2, t0, t1)
+
+        y = []
+        for t in range(PACK):
+            cols = slice(t * P, (t + 1) * P)
+            y_ps = psum.tile([P, S], F32, name=f"y_ps{t}", tag=f"bank{t}")
+            nc.tensor.matmul_mx(out=y_ps[:], lhsT=w1_d[:, cols].bitcast(FP8X4), lhsT_scale=ws_d[:, cols],
+                                rhs=xq_w[:].bitcast(FP8X4), rhs_scale=xq_s[:], start=True, stop=False)
+            nc.tensor.matmul_mx(out=y_ps[:], lhsT=w2_d[:, cols].bitcast(FP8X4), lhsT_scale=ws_d[4:P, cols],
+                                rhs=xt_w[:].bitcast(FP8X4), rhs_scale=xt_s[:], start=False, stop=True)
+            y_t = keep.tile([P, S], F32, name=f"y{t}")
+            nc.vector.tensor_scalar(y_t[:], y_ps[:], gs_t[:, t : t + 1], None, ALU.mult)
+            y.append(y_t)
+        ds = [keep.tile([P, S], F32, name=f"ds{t}") for t in range(PACK)]
+        for t in range(PACK):
+            nc.vector.tensor_copy(ds[t][:], y[t][:])
+
+        xc_w, xc_s = pick(cand_t, C, "xc", "first")
+        bias_t = keep.tile([P, C // P], F32)
+        nc.vector.scalar_tensor_tensor(bias_t[:], sl_t[:], -1.0, th_t[:], ALU.mult, ALU.mult)
+
+        pa = keep.tile([P, PACK, W], F32, tag="fetch")
+        for t in range(PACK):
+            nc.scalar.activation(pa[:, t, :], y[t][:].indirect(n2_t[:]), ACT.Copy)
+        for t in range(PACK):
+            nc.scalar.activation(ds[t][:].indirect(n1_t[:]), pa[:, t, :], ACT.Copy)
+
+        s = [keep.tile([P, S], F32, name=f"s{c}") for c in range(C // P)]
+        page = [keep.tile([P, U], F32, name=f"page{c}") for c in range(C // P)]
+        later = None
+
+        for g, (j0, j1) in enumerate(PIECES):
+            n = j1 - j0
+            if g == 0:
+                first = keep.tile([P, PACK, n], F32, name="fetched_first")
+                fetched = first[:]
+            else:
+                if later is None:
+                    later = keep.tile([P, PACK * (S - j0)], F32, name="fetched_later", tag="fetch")
+                base = PACK * (j0 - PIECES[1][0])
+                fetched = later[:, base : base + PACK * n].rearrange("p (t j) -> p t j", t=PACK)
+            z_rows = keep.tile([P, PACK, n], BF16, name=f"z_rows{g}")
+            for t in range(PACK):
+                nc.scalar.activation(fetched[:, t, :], ds[t][:].indirect(part(n3_t, j0, j1)), ACT.Copy)
+                nc.vector.scalar_tensor_tensor(z_rows[:, t, :], fetched[:, t, :], -0.5, ds[t][:, j0:j1], ALU.mult, ALU.add)
+            z_k = keep.tile([P, n, PACK], BF16, name=f"z_k{g}", align_bytes=64)
+            nc.vector.tensor_copy(z_k[:].rearrange("p (j i) t -> p j t i", i=4),
+                                  z_rows[:].rearrange("p t (j i) -> p j t i", i=4))
+            z_w = keep.tile([P, n], U32, name=f"z_w{g}", align_bytes=64)
+            z_s = keep.tile([P, n], U8, name=f"z_s{g}", align_bytes=64)
+            nc.vector.quantize_mx(out=z_w[:].bitcast(FP8X4), scales=z_s[:], in_=z_k[:].rearrange("p j t -> p (j t)"))
+            for c in range(C // P):
+                cols = slice(c * P, (c + 1) * P)
+                s_ps = psum.tile([P, n], F32, name=f"s_ps{g}_{c}", tag=f"bank{PACK * ((g + 1) % 2) + c}")
+                nc.tensor.matmul_mx(out=s_ps[:], lhsT=xc_w[:, cols].bitcast(FP8X4), lhsT_scale=xc_s[:, cols],
+                                    rhs=z_w[:].bitcast(FP8X4), rhs_scale=z_s[:], start=True, stop=True)
+                nc.vector.tensor_scalar(s[c][:, j0:j1], s_ps[:], 0.0625, None, ALU.mult)
+
+        def put_s(c, j0, j1):
+            nc.scalar.activation(page[c][:].indirect(part(n4_t, j0, j1)), s[c][:, j0:j1], ACT.Copy)
+
+        for j0, j1 in PIECES[:-1]:
+            for c in range(C // P):
+                put_s(c, j0, j1)
+        for c in range(C // P):
+            sg = keep.tile([P, S], F32, name=f"sg{c}")
+            for j0 in (0, HALF):
+                nc.scalar.activation(sg[:, j0 : j0 + HALF], s[c][:].indirect(part(n6_t, j0, j0 + HALF)), ACT.Sigmoid,
+                                     bias=bias_t[:, c : c + 1], scale=sl_t[:, c : c + 1])
+            st = keep.tile([P, S], F32, name=f"st{c}")
+            nc.vector.tensor_tensor(st[:], s[c][:], sg[:], ALU.mult)
+            put_s(c, *PIECES[-1])
+            nc.scalar.activation(page[c][:].indirect(n5_t[:]), st[:], ACT.Copy)
+            nc.sync.dma_start(out[c * P : (c + 1) * P, :], page[c][:])

@@ -32,6 +32,7 @@ def tile_picked_dttzcksetepag_none_p_kernel(
 
     with ExitStack() as ctx:
         keep = ctx.enter_context(tc.tile_pool(name="keep", bufs=1))
+        reuse = ctx.enter_context(tc.tile_pool(name="reuse", bufs=1))
         psum = ctx.enter_context(tc.psum_pool(name="psum", bufs=1))
 
         def load_list(src, name):
@@ -52,12 +53,18 @@ def tile_picked_dttzcksetepag_none_p_kernel(
         def part(lst, j0, j1):
             return lst[:, j0 // LIST_COL : j1 // LIST_COL]
 
+        warm_in = keep.tile([P, 1], F32)
+        warm_out = keep.tile([P, 1], F32)
+        nc.gpsimd.memset(warm_in[:], 0.0)
+        nc.scalar.activation(warm_out[:], warm_in[:], ACT.Sigmoid)
+
         xs = keep.tile([P, T], U8, align_bytes=64)
         ws = keep.tile([P, H], U8, align_bytes=64)
         nc.vector.memset(xs[:].bitcast(I32), 0)
         nc.vector.memset(ws[:].bitcast(I32), 0)
 
-        load_scale_rows(nc.sync, xs, x_scales, 0, range(QUADS))
+        load_scale_rows(nc.sync, xs, x_scales, 0, range(2))
+        load_scale_rows(nc.scalar, xs, x_scales, 0, range(2, QUADS))
         offs_t = load_list(offs, "offs_t")
         two_t = load_list(two, "two_t")
         gs_t = keep.tile([P, PACK], F32)
@@ -81,72 +88,71 @@ def tile_picked_dttzcksetepag_none_p_kernel(
             nc.sync.dma_start(sl_t[:], sl.rearrange("(c p) o -> p (c o)", p=P))
             nc.sync.dma_start(th_t[:], th.rearrange("(c p) o -> p (c o)", p=P))
 
-        def pick(lst, n, name, tag):
-            scales = keep.tile([P, n], U8, name=name + "_scales", tag=tag + "_scales", align_bytes=64)
-            words = keep.tile([P, n], U32, name=name + "_words", tag=tag + "_words", align_bytes=64)
+        def pick(lst, words, scales):
             nc.vector.tensor_copy(scales[:], xs[:].indirect(lst[:]))
             nc.vector.tensor_copy(words[:], xw[:].indirect(lst[:]))
-            return words, scales
 
-        xq_w, xq_s = pick(offs_t, S, "xq", "first")
-        xt_w, xt_s = pick(two_t, S, "xt", "second")
+        xq_w = keep.tile([P, S], U32, align_bytes=64)
+        xq_s = keep.tile([P, S], U8, align_bytes=64)
+        xt_w = keep.tile([P, S], U32, align_bytes=64)
+        xt_s = keep.tile([P, S], U8, align_bytes=64)
+        pick(offs_t, xq_w, xq_s)
+        pick(two_t, xt_w, xt_s)
 
         ws_d = keep.tile([P, H], U8, align_bytes=64)
         w1_d = keep.tile([P, H], U32, align_bytes=64)
         w2_d = keep.tile([P, H], U32, align_bytes=64)
 
         def deal(copy, dst, src, t0, t1):
-            copy(dst[:].rearrange("p (t m) -> p t m", t=PACK)[:, t0:t1, :], src[:].rearrange("p (m t) -> p t m", t=PACK)[:, t0:t1, :])
+            copy(dst[:].rearrange("p (t m i) -> p m t i", t=PACK, i=4)[:, :, t0:t1, :],
+                 src[:].rearrange("p (m i t) -> p m t i", t=PACK, i=4)[:, :, t0:t1, :])
 
-        nc.scalar.copy(w1_d[:].rearrange("p (t m) -> p m t", t=PACK), w1[:].rearrange("p (m t) -> p m t", t=PACK))
         for t0, t1 in ((0, 1), (1, PACK)):
             deal(nc.vector.tensor_copy, ws_d, ws, t0, t1)
-            deal(nc.scalar.copy, w2_d, w2, t0, t1)
+            deal(nc.scalar.copy, w1_d, w1, t0, t1)
+            deal(nc.vector.tensor_copy, w2_d, w2, t0, t1)
 
         y = []
         for t in range(PACK):
             cols = slice(t * P, (t + 1) * P)
             y_ps = psum.tile([P, S], F32, name=f"y_ps{t}", tag=f"bank{t}")
-            nc.tensor.matmul_mx(out=y_ps[:], lhsT=w1_d[:, cols].bitcast(FP8X4), lhsT_scale=ws_d[:, cols],
-                                rhs=xq_w[:].bitcast(FP8X4), rhs_scale=xq_s[:], start=True, stop=False)
             nc.tensor.matmul_mx(out=y_ps[:], lhsT=w2_d[:, cols].bitcast(FP8X4), lhsT_scale=ws_d[4:P, cols],
-                                rhs=xt_w[:].bitcast(FP8X4), rhs_scale=xt_s[:], start=False, stop=True)
-            y_t = keep.tile([P, S], F32, name=f"y{t}")
+                                rhs=xt_w[:].bitcast(FP8X4), rhs_scale=xt_s[:], start=True, stop=False)
+            nc.tensor.matmul_mx(out=y_ps[:], lhsT=w1_d[:, cols].bitcast(FP8X4), lhsT_scale=ws_d[:, cols],
+                                rhs=xq_w[:].bitcast(FP8X4), rhs_scale=xq_s[:], start=False, stop=True)
+            y_t = reuse.tile([P, S], F32, name=f"y{t}", offset=4 * S * (PACK - 1 - t), align_bytes=64) if t == PACK - 1 else keep.tile([P, S], F32, name=f"y{t}")
             nc.vector.tensor_scalar(y_t[:], y_ps[:], gs_t[:, t : t + 1], None, ALU.mult)
             y.append(y_t)
         ds = [keep.tile([P, S], F32, name=f"ds{t}") for t in range(PACK)]
         for t in range(PACK):
             nc.vector.tensor_copy(ds[t][:], y[t][:])
 
-        xc_w, xc_s = pick(cand_t, C, "xc", "first")
+        xc_s = reuse.tile([P, C], U8, offset=0, align_bytes=64)
+        xc_w = reuse.tile([P, C], U32, offset=C, align_bytes=64)
+        pick(cand_t, xc_w, xc_s)
         bias_t = keep.tile([P, C // P], F32)
         nc.vector.scalar_tensor_tensor(bias_t[:], sl_t[:], -1.0, th_t[:], ALU.mult, ALU.mult)
 
-        pa = keep.tile([P, PACK, W], F32, tag="fetch")
+        pa_first = keep.tile([P, PACK - 1, W], F32, tag="fetch")
+        pa_last = keep.tile([P, W], F32)
+        pa = [pa_first[:, t, :] for t in range(PACK - 1)] + [pa_last[:]]
         for t in range(PACK):
-            nc.scalar.activation(pa[:, t, :], y[t][:].indirect(n2_t[:]), ACT.Copy)
+            nc.scalar.activation(pa[t], y[t][:].indirect(n2_t[:]), ACT.Copy)
         for t in range(PACK):
-            nc.scalar.activation(ds[t][:].indirect(n1_t[:]), pa[:, t, :], ACT.Copy)
+            nc.scalar.activation(ds[t][:].indirect(n1_t[:]), pa[t], ACT.Copy)
 
         s = [keep.tile([P, S], F32, name=f"s{c}") for c in range(C // P)]
         page = [keep.tile([P, U], F32, name=f"page{c}") for c in range(C // P)]
-        later = None
+        fetch_all = keep.tile([P, PACK * S], F32, tag="fetch")
 
         for g, (j0, j1) in enumerate(PIECES):
             n = j1 - j0
-            if g == 0:
-                first = keep.tile([P, PACK, n], F32, name="fetched_first")
-                fetched = first[:]
-            else:
-                if later is None:
-                    later = keep.tile([P, PACK * (S - j0)], F32, name="fetched_later", tag="fetch")
-                base = PACK * (j0 - PIECES[1][0])
-                fetched = later[:, base : base + PACK * n].rearrange("p (t j) -> p t j", t=PACK)
-            z_rows = keep.tile([P, PACK, n], BF16, name=f"z_rows{g}")
+            fetched = fetch_all[:, PACK * j0 : PACK * j1].rearrange("p (t j) -> p t j", t=PACK)
+            z_rows = keep.tile([P, PACK, n], BF16, name=f"z_rows{g}", tag=f"z{g}", align_bytes=64)
             for t in range(PACK):
                 nc.scalar.activation(fetched[:, t, :], ds[t][:].indirect(part(n3_t, j0, j1)), ACT.Copy)
                 nc.vector.scalar_tensor_tensor(z_rows[:, t, :], fetched[:, t, :], -0.5, ds[t][:, j0:j1], ALU.mult, ALU.add)
-            z_k = keep.tile([P, n, PACK], BF16, name=f"z_k{g}", align_bytes=64)
+            z_k = keep.tile([P, n, PACK], BF16, name=f"z_k{g}", tag=f"z{g + 1}", align_bytes=64)
             nc.vector.tensor_copy(z_k[:].rearrange("p (j i) t -> p j t i", i=4),
                                   z_rows[:].rearrange("p t (j i) -> p j t i", i=4))
             z_w = keep.tile([P, n], U32, name=f"z_w{g}", align_bytes=64)
@@ -165,13 +171,20 @@ def tile_picked_dttzcksetepag_none_p_kernel(
         for j0, j1 in PIECES[:-1]:
             for c in range(C // P):
                 put_s(c, j0, j1)
+        st = []
+
+        def put_st(c):
+            nc.scalar.activation(page[c][:].indirect(n5_t[:]), st[c][:], ACT.Copy)
+            nc.sync.dma_start(out[c * P : (c + 1) * P, :], page[c][:])
+
         for c in range(C // P):
             sg = keep.tile([P, S], F32, name=f"sg{c}")
             for j0 in (0, HALF):
                 nc.scalar.activation(sg[:, j0 : j0 + HALF], s[c][:].indirect(part(n6_t, j0, j0 + HALF)), ACT.Sigmoid,
                                      bias=bias_t[:, c : c + 1], scale=sl_t[:, c : c + 1])
-            st = keep.tile([P, S], F32, name=f"st{c}")
-            nc.vector.tensor_tensor(st[:], s[c][:], sg[:], ALU.mult)
+            st.append(keep.tile([P, S], F32, name=f"st{c}"))
+            nc.vector.tensor_tensor(st[c][:], s[c][:], sg[:], ALU.mult)
             put_s(c, *PIECES[-1])
-            nc.scalar.activation(page[c][:].indirect(n5_t[:]), st[:], ACT.Copy)
-            nc.sync.dma_start(out[c * P : (c + 1) * P, :], page[c][:])
+            if c > 0:
+                put_st(c - 1)
+        put_st(C // P - 1)

from contextlib import ExitStack

import concourse.mybir as mybir

K, T, S, H, W, C, U = 512, 2048, 256, 512, 128, 512, 512
FLOPS = 2 * K * S * (2 * H + C)

F32 = mybir.dt.float32
BF16 = mybir.dt.bfloat16
I32 = mybir.dt.int32
U32 = mybir.dt.uint32
U16 = mybir.dt.uint16
U8 = mybir.dt.uint8
FP8X4 = mybir.dt.float8_e4m3fn_x4
ALU = mybir.AluOpType
ACT = mybir.ActivationFunctionType

P = 128
PACK = 4
QUADS = 4
QUAD = 32
HALF = S // 2
LIST_COL = 16
PIECES = ((0, 128), (128, 256))


def tile_picked_dttzcksetepag_none_p_kernel(
    tc, x_words, x_scales, w1_words, w1_scales, w2_words, w2_scales, gs, sl, th,
    offs, two, n1, n2, n3, cand, n4, n5, n6, out,
):
    nc = tc.nc

    with ExitStack() as ctx:
        keep = ctx.enter_context(tc.tile_pool(name="keep", bufs=1))
        reuse = ctx.enter_context(tc.tile_pool(name="reuse", bufs=1))
        psum = ctx.enter_context(tc.psum_pool(name="psum", bufs=1))

        def load_list(src, name):
            tile = keep.tile(list(src.shape), U16, name=name)
            nc.sync.dma_start(tile[:], src)
            return tile

        def load_words(src, name):
            tile = keep.tile([P, src.shape[2]], U32, name=name, align_bytes=64)
            nc.sync.dma_start(tile[:].bitcast(I32), src[0].rearrange("p n t -> p (n t)").bitcast(I32))
            return tile

        def load_scale_rows(queue, tile, src, first, quads):
            for q in quads:
                rows = tile[QUAD * q + first : QUAD * q + first + 4, :]
                queue.dma_start(rows.bitcast(I32), src[0, 4 * q : 4 * q + 4, :].bitcast(I32))

        def part(lst, j0, j1):
            return lst[:, j0 // LIST_COL : j1 // LIST_COL]

        warm_in = keep.tile([P, 1], F32)
        warm_out = keep.tile([P, 1], F32)
        nc.gpsimd.memset(warm_in[:], 0.0)
        nc.scalar.activation(warm_out[:], warm_in[:], ACT.Sigmoid)

        xs = keep.tile([P, T], U8, align_bytes=64)
        ws = keep.tile([P, H], U8, align_bytes=64)
        nc.vector.memset(xs[:].bitcast(I32), 0)
        nc.vector.memset(ws[:].bitcast(I32), 0)

        load_scale_rows(nc.sync, xs, x_scales, 0, range(2))
        load_scale_rows(nc.scalar, xs, x_scales, 0, range(2, QUADS))
        offs_t = load_list(offs, "offs_t")
        two_t = load_list(two, "two_t")
        gs_t = keep.tile([P, PACK], F32)
        nc.sync.dma_start(gs_t[:], gs.rearrange("(p t) o -> p (t o)", t=PACK))
        xw = load_words(x_words, "xw")
        load_scale_rows(nc.sync, ws, w1_scales, 0, range(QUADS))
        w1 = load_words(w1_words, "w1")
        load_scale_rows(nc.sync, ws, w2_scales, 4, range(1))
        load_scale_rows(nc.gpsimd, ws, w2_scales, 4, range(1, QUADS))
        w2 = load_words(w2_words, "w2")
        n2_t = load_list(n2, "n2_t")
        n1_t = load_list(n1, "n1_t")
        n3_t = load_list(n3, "n3_t")
        cand_t = load_list(cand, "cand_t")
        n4_t = load_list(n4, "n4_t")
        n6_t = load_list(n6, "n6_t")
        n5_t = load_list(n5, "n5_t")
        sl_t = keep.tile([P, C // P], F32)
        th_t = keep.tile([P, C // P], F32)
        with nc.allow_non_contiguous_dma(reason="one value a partition for each block of rows"):
            nc.sync.dma_start(sl_t[:], sl.rearrange("(c p) o -> p (c o)", p=P))
            nc.sync.dma_start(th_t[:], th.rearrange("(c p) o -> p (c o)", p=P))

        def pick(lst, words, scales):
            nc.vector.tensor_copy(scales[:], xs[:].indirect(lst[:]))
            nc.vector.tensor_copy(words[:], xw[:].indirect(lst[:]))

        xq_w = keep.tile([P, S], U32, align_bytes=64)
        xq_s = keep.tile([P, S], U8, align_bytes=64)
        xt_w = keep.tile([P, S], U32, align_bytes=64)
        xt_s = keep.tile([P, S], U8, align_bytes=64)
        pick(offs_t, xq_w, xq_s)
        pick(two_t, xt_w, xt_s)

        ws_d = keep.tile([P, H], U8, align_bytes=64)
        w1_d = keep.tile([P, H], U32, align_bytes=64)
        w2_d = keep.tile([P, H], U32, align_bytes=64)

        def deal(copy, dst, src, t0, t1):
            copy(dst[:].rearrange("p (t m i) -> p m t i", t=PACK, i=4)[:, :, t0:t1, :],
                 src[:].rearrange("p (m i t) -> p m t i", t=PACK, i=4)[:, :, t0:t1, :])

        for t0, t1 in ((0, 1), (1, PACK)):
            deal(nc.vector.tensor_copy, ws_d, ws, t0, t1)
            deal(nc.scalar.copy, w1_d, w1, t0, t1)
            deal(nc.vector.tensor_copy, w2_d, w2, t0, t1)

        y = []
        for t in range(PACK):
            cols = slice(t * P, (t + 1) * P)
            y_ps = psum.tile([P, S], F32, name=f"y_ps{t}", tag=f"bank{t}")
            nc.tensor.matmul_mx(out=y_ps[:], lhsT=w2_d[:, cols].bitcast(FP8X4), lhsT_scale=ws_d[4:P, cols],
                                rhs=xt_w[:].bitcast(FP8X4), rhs_scale=xt_s[:], start=True, stop=False)
            nc.tensor.matmul_mx(out=y_ps[:], lhsT=w1_d[:, cols].bitcast(FP8X4), lhsT_scale=ws_d[:, cols],
                                rhs=xq_w[:].bitcast(FP8X4), rhs_scale=xq_s[:], start=False, stop=True)
            y_t = reuse.tile([P, S], F32, name=f"y{t}", offset=4 * S * (PACK - 1 - t), align_bytes=64) if t == PACK - 1 else keep.tile([P, S], F32, name=f"y{t}")
            nc.vector.tensor_scalar(y_t[:], y_ps[:], gs_t[:, t : t + 1], None, ALU.mult)
            y.append(y_t)
        ds = [keep.tile([P, S], F32, name=f"ds{t}") for t in range(PACK)]
        for t in range(PACK):
            nc.vector.tensor_copy(ds[t][:], y[t][:])

        xc_s = reuse.tile([P, C], U8, offset=0, align_bytes=64)
        xc_w = reuse.tile([P, C], U32, offset=C, align_bytes=64)
        pick(cand_t, xc_w, xc_s)
        bias_t = keep.tile([P, C // P], F32)
        nc.vector.scalar_tensor_tensor(bias_t[:], sl_t[:], -1.0, th_t[:], ALU.mult, ALU.mult)

        pa_first = keep.tile([P, PACK - 1, W], F32, tag="fetch")
        pa_last = keep.tile([P, W], F32)
        pa = [pa_first[:, t, :] for t in range(PACK - 1)] + [pa_last[:]]
        for t in range(PACK):
            nc.scalar.activation(pa[t], y[t][:].indirect(n2_t[:]), ACT.Copy)
        for t in range(PACK):
            nc.scalar.activation(ds[t][:].indirect(n1_t[:]), pa[t], ACT.Copy)

        s = [keep.tile([P, S], F32, name=f"s{c}") for c in range(C // P)]
        page = [keep.tile([P, U], F32, name=f"page{c}") for c in range(C // P)]
        fetch_all = keep.tile([P, PACK * S], F32, tag="fetch")

        for g, (j0, j1) in enumerate(PIECES):
            n = j1 - j0
            fetched = fetch_all[:, PACK * j0 : PACK * j1].rearrange("p (t j) -> p t j", t=PACK)
            z_rows = keep.tile([P, PACK, n], BF16, name=f"z_rows{g}", tag=f"z{g}", align_bytes=64)
            for t in range(PACK):
                nc.scalar.activation(fetched[:, t, :], ds[t][:].indirect(part(n3_t, j0, j1)), ACT.Copy)
                nc.vector.scalar_tensor_tensor(z_rows[:, t, :], fetched[:, t, :], -0.5, ds[t][:, j0:j1], ALU.mult, ALU.add)
            z_k = keep.tile([P, n, PACK], BF16, name=f"z_k{g}", tag=f"z{g + 1}", align_bytes=64)
            nc.vector.tensor_copy(z_k[:].rearrange("p (j i) t -> p j t i", i=4),
                                  z_rows[:].rearrange("p t (j i) -> p j t i", i=4))
            z_w = keep.tile([P, n], U32, name=f"z_w{g}", align_bytes=64)
            z_s = keep.tile([P, n], U8, name=f"z_s{g}", align_bytes=64)
            nc.vector.quantize_mx(out=z_w[:].bitcast(FP8X4), scales=z_s[:], in_=z_k[:].rearrange("p j t -> p (j t)"))
            for c in range(C // P):
                cols = slice(c * P, (c + 1) * P)
                s_ps = psum.tile([P, n], F32, name=f"s_ps{g}_{c}", tag=f"bank{PACK * ((g + 1) % 2) + c}")
                nc.tensor.matmul_mx(out=s_ps[:], lhsT=xc_w[:, cols].bitcast(FP8X4), lhsT_scale=xc_s[:, cols],
                                    rhs=z_w[:].bitcast(FP8X4), rhs_scale=z_s[:], start=True, stop=True)
                nc.vector.tensor_scalar(s[c][:, j0:j1], s_ps[:], 0.0625, None, ALU.mult)

        def put_s(c, j0, j1):
            nc.scalar.activation(page[c][:].indirect(part(n4_t, j0, j1)), s[c][:, j0:j1], ACT.Copy)

        for j0, j1 in PIECES[:-1]:
            for c in range(C // P):
                put_s(c, j0, j1)
        st = []

        def put_st(c):
            nc.scalar.activation(page[c][:].indirect(n5_t[:]), st[c][:], ACT.Copy)
            nc.sync.dma_start(out[c * P : (c + 1) * P, :], page[c][:])

        for c in range(C // P):
            sg = keep.tile([P, S], F32, name=f"sg{c}")
            for j0 in (0, HALF):
                nc.scalar.activation(sg[:, j0 : j0 + HALF], s[c][:].indirect(part(n6_t, j0, j0 + HALF)), ACT.Sigmoid,
                                     bias=bias_t[:, c : c + 1], scale=sl_t[:, c : c + 1])
            st.append(keep.tile([P, S], F32, name=f"st{c}"))
            nc.vector.tensor_tensor(st[c][:], s[c][:], sg[:], ALU.mult)
            put_s(c, *PIECES[-1])
            if c > 0:
                put_st(c - 1)
        put_st(C // P - 1)
